import numpy as np
import ml_dtypes


def mxq(x, axis, fmt="e4m3"):
    dtype, down = {"e4m3": (ml_dtypes.float8_e4m3fn, 7), "e5m2": (ml_dtypes.float8_e5m2, 14)}[fmt]
    v = np.moveaxis(np.asarray(x, np.float32).astype(ml_dtypes.bfloat16).astype(np.float64), axis, -1)
    blocks = v.reshape(v.shape[:-1] + (-1, 32))
    amax = np.abs(blocks).max(-1, keepdims=True)
    byte = np.maximum(np.where(amax > 0, np.frexp(amax)[1] - 1 + 127, 0) - down, 1)
    scale = np.exp2(byte - 127.0)
    codes = (blocks / scale).astype(np.float32).astype(dtype).astype(np.float64)
    return np.moveaxis((codes * scale).reshape(v.shape), -1, axis)


WIDE = False


def mx_kscale(k):
    if not WIDE:
        return np.ones(k)
    levels = np.array([10, -10, 5, -5, 0])
    if k % 512:
        return np.exp2(np.random.permutation(np.resize(levels, k // 32))).repeat(32)
    a = np.empty((k // 512, 16))
    for p in range(k // 512):
        a[p, :8] = np.random.permutation(np.resize(levels, 8))
        for g in range(8):
            far = levels[np.abs(levels - a[p, g]) >= 10]
            a[p, g + 8] = far[np.random.randint(len(far))]
    return np.exp2(a.ravel()).repeat(32)


def f64(x):
    return np.asarray(x).astype(np.float64)


def striped(idx):
    return np.tile(idx.reshape(-1, 16).T, (8, 1)).astype(np.uint16)


def unstriped(offs):
    return offs[:16].T.reshape(-1).astype(np.int64)


def silu(v):
    return v / (1.0 + np.exp(-np.maximum(v, -700.0)))


K, T, E, C, H, N = 1536, 512, 4, 256, 512, 128


def by_expert(wq, xq):
    return np.concatenate([wq[e].T @ xq[:, e * C:(e + 1) * C] for e in range(E)], axis=1)


def setup_inputs():
    n = np.random.standard_normal
    s = mx_kscale(K)[:, None]
    u = mx_kscale(H)
    first = np.random.permutation(np.repeat(np.arange(E), T // E))
    second = (first + 1 + np.random.permutation(np.repeat(np.arange(E - 1), -(-T // (E - 1)))[:T])) % E
    while np.bincount(second, minlength=E).max() != T // E:
        load = np.bincount(second, minlength=E); hi, lo = int(load.argmax()), int(load.argmin())
        t = np.flatnonzero((second == hi) & (first != lo))[0]; second[t] = lo
    slot_token = np.empty(E * C, np.int64); pos = np.empty((2, T), np.int64); fill = np.zeros(E, np.int64)
    place = np.stack([np.random.permutation(C) for _ in range(E)])
    for r, deal in enumerate((first, second)):
        for t in np.random.permutation(T):
            e = deal[t]; j = e * C + place[e, fill[e]]; fill[e] += 1; slot_token[j] = t; pos[r, t] = j
    g = np.random.uniform(0.2, 0.8, T)
    return {
        "xT": (n((K, T)) * s).astype(np.float32),
        "w1": (n((E, K, H)) / np.sqrt(K) / s[None]).astype(np.float32),
        "w3": (n((E, K, H)) / np.sqrt(K) / s[None] * u[None, None, :]).astype(np.float32),
        "w2": (n((E, H, N)) / np.sqrt(H) / u[None, :, None]).astype(np.float32),
        "gate": np.stack([np.tile(g, (N, 1)), np.tile(1.0 - g, (N, 1))]).astype(np.float32),
        "offs": striped(slot_token),
        "pos1": striped(pos[0]),
        "pos2": striped(pos[1]),
    }


def reference(xT, w1, w3, w2, gate, offs, pos1, pos2):
    idx = unstriped(offs)
    xq = mxq(f64(xT)[:, idx], 0, "e4m3")
    h = silu(by_expert(mxq(f64(w1), 1, "e4m3"), xq))
    h = h * by_expert(mxq(f64(w3), 1, "e4m3"), xq)
    y = by_expert(mxq(f64(w2), 1, "e4m3"), mxq(h, 0, "e4m3"))
    return f64(gate[0]) * y[:, unstriped(pos1)] + f64(gate[1]) * y[:, unstriped(pos2)]

@@ -1,0 +1,241 @@
+import concourse.mybir as mybir
+
+K, T, E, C, H, N = 1536, 512, 4, 256, 512, 128
+FLOPS = 2 * E * C * H * (2 * K + N)
+
+F32 = mybir.dt.float32
+BF16 = mybir.dt.bfloat16
+U32 = mybir.dt.uint32
+U16 = mybir.dt.uint16
+U8 = mybir.dt.uint8
+FP8X4 = mybir.dt.float8_e4m3fn_x4
+SILU = mybir.ActivationFunctionType.Silu
+MULT = mybir.AluOpType.mult
+ADD = mybir.AluOpType.add
+
+P = 128
+J = 4
+PASSES = K // (P * J)
+HALF = 128
+PIECES = ((0, 384), (384, 704), (704, 1024))
+RAW_BUFS = 12
+SPLIT_M = 88
+VECTOR_CHUNKS = (6, 8, 10, 12, 14, 17, 19, 21)
+
+
+def tile_routed_moe_kernel(tc, xT, w1, w3, w2, gate, offs, pos1, pos2, out):
+    nc = tc.nc
+    with (
+        tc.tile_pool(name="keep", bufs=1) as keep,
+        tc.tile_pool(name="raw", bufs=RAW_BUFS) as rawp,
+        tc.tile_pool(name="grouped", bufs=8) as grp,
+        tc.tile_pool(name="codes", bufs=4) as codes,
+        tc.tile_pool(name="hid", bufs=4) as hid,
+        tc.psum_pool(name="pa", bufs=3) as pa,
+        tc.psum_pool(name="pb", bufs=3) as pb,
+        tc.psum_pool(name="py", bufs=2) as py,
+    ):
+        offs_sb = keep.tile([P, E * C // 16], U16, name="offs_sb")
+        pos1_sb = keep.tile([P, T // 16], U16, name="pos1_sb")
+        pos2_sb = keep.tile([P, T // 16], U16, name="pos2_sb")
+        gate_sb = keep.tile([P, 2, T], F32, name="gate_sb")
+        y_sb = keep.tile([P, E * C], F32, name="y_sb")
+        xcodes = [keep.tile([P, T], U32, name="xc%d" % g, align_bytes=64) for g in range(PASSES)]
+        xscale = keep.tile([P, T], U8, name="xscale", align_bytes=64)
+        scodes = [keep.tile([P, E * C], U32, name="sc%d" % g, align_bytes=64) for g in range(PASSES)]
+        sscale = keep.tile([P, E * C], U8, name="sscale", align_bytes=64)
+        w2codes = keep.tile([P, E * N], U32, name="w2codes", align_bytes=64)
+        w2scale = keep.tile([P, E * N], U8, name="w2scale", align_bytes=64)
+        warm = keep.tile([P, 8], F32, name="warm")
+
+        nc.gpsimd.memset(warm[:], 0.0)
+        nc.scalar.activation(warm[:], warm[:], SILU)
+        nc.gpsimd.memset(xscale[:], 0)
+
+        chunks = [(e, w, g) for e in range(E) for w in range(2) for g in range(PASSES)]
+        raws = {}
+
+        def load_w(i):
+            e, w, g = chunks[i]
+            raw = rawp.tile([P, J, H], F32, name="raw")
+            src = (w1, w3)[w][e].rearrange("(g p j) c -> g p j c", p=P, j=J)[g]
+            nc.sync.dma_start(out=raw[:], in_=src)
+            raws[i] = raw
+
+        nc.sync.dma_start(offs_sb[:], offs)
+        xraw = []
+        for g in range(PASSES):
+            raw = rawp.tile([P, J, T], F32, name="raw")
+            nc.sync.dma_start(out=raw[:], in_=xT.rearrange("(g p j) n -> g p j n", p=P, j=J)[g])
+            xraw.append(raw)
+        for i in range(RAW_BUFS - PASSES):
+            load_w(i)
+        loaded = RAW_BUFS - PASSES
+
+        w2raw = []
+
+        def load_w2(e0):
+            raw = keep.tile([P, 2, J, N], F32, name="w2raw%d" % e0)
+            nc.sync.dma_start(out=raw[:], in_=w2[e0 : e0 + 2].rearrange("e (p j) n -> p e j n", j=J))
+            w2raw.append(raw)
+
+        def w2_prepare(e0):
+            raw = w2raw[e0 // 2]
+            g4 = keep.tile([P, 2 * N * J], BF16, name="w2g%d" % e0, align_bytes=64)
+            for k in range(2):
+                nc.scalar.copy(
+                    g4[:, k * N * J : (k + 1) * N * J].rearrange("p (c i j) -> p c j i", i=4, j=J),
+                    raw[:, k].rearrange("p j (c i) -> p c j i", i=4),
+                )
+            cols = slice(e0 * N, (e0 + 2) * N)
+            nc.vector.quantize_mx(out=w2codes[:, cols].bitcast(FP8X4), scales=w2scale[:, cols], in_=g4[:])
+
+        for g in range(PASSES):
+            g4 = grp.tile([P, T * J], BF16, name="xg", tag="g4", align_bytes=64)
+            dst = g4[:].rearrange("p (c i j) -> p c j i", i=4, j=J)
+            src = xraw[g][:].rearrange("p j (c i) -> p c j i", i=4)
+            if g == 0:
+                nc.vector.tensor_copy(dst, src)
+            else:
+                nc.scalar.copy(dst, src)
+            nc.vector.quantize_mx(out=xcodes[g][:].bitcast(FP8X4), scales=xscale[4 * g : P, :], in_=g4[:])
+            for a, b in PIECES:
+                nc.vector.tensor_copy(scodes[g][:, a:b], xcodes[g][:].indirect(offs_sb[:, a // 16 : b // 16]))
+        for a, b in PIECES:
+            nc.vector.tensor_copy(sscale[:, a:b], xscale[:].indirect(offs_sb[:, a // 16 : b // 16]))
+
+        grouped = {}
+        wq = {}
+
+        def regroup(i):
+            g4 = grp.tile([P, H * J], BF16, name="wg", tag="g4", align_bytes=64)
+            dst = g4[:].rearrange("p (t m j) -> p m j t", t=4, j=J)
+            src = raws.pop(i)[:].rearrange("p j (m t) -> p m j t", t=4)
+            if i == len(chunks) - 1:
+                nc.vector.tensor_copy(dst[:, :SPLIT_M], src[:, :SPLIT_M])
+                nc.scalar.copy(dst[:, SPLIT_M:], src[:, SPLIT_M:])
+            elif i in VECTOR_CHUNKS:
+                nc.vector.tensor_copy(dst, src)
+            else:
+                nc.scalar.copy(dst, src)
+            grouped[i] = g4
+
+        def quantise(i):
+            e, w, g = chunks[i]
+            if g == 0:
+                wc = codes.tile([P, PASSES, H], U32, name="wc", align_bytes=64)
+                ws = codes.tile([P, PASSES, H], U8, name="ws", align_bytes=64)
+                wq[e, w] = (wc, ws)
+            wc, ws = wq[e, w]
+            nc.vector.quantize_mx(out=wc[:, g].bitcast(FP8X4), scales=ws[:, g], in_=grouped.pop(i)[:])
+
+        banks = {}
+
+        def multiply(e, w):
+            wc, ws = wq.pop((e, w))
+            for h in range(2):
+                bank = (pa, pb)[w].tile([P, 4, HALF], F32, name="bank%d" % w)
+                cols = slice(e * C + h * HALF, e * C + (h + 1) * HALF)
+                for t in range(4):
+                    rows = slice(t * P, (t + 1) * P)
+                    for g in range(PASSES):
+                        nc.tensor.matmul_mx(
+                            out=bank[:, t],
+                            lhsT=wc[:, g, rows].bitcast(FP8X4),
+                            lhsT_scale=ws[:, g, rows],
+                            rhs=scodes[g][:, cols].bitcast(FP8X4),
+                            rhs_scale=sscale[4 * g : P, cols],
+                            start=(g == 0),
+                            stop=(g == PASSES - 1),
+                        )
+                banks[e, w, h] = bank
+
+        silus = {}
+        hcodes = {}
+
+        def activate(e, after):
+            bias = hid.tile([P, 1], F32, name="bias")
+            nc.gpsimd.tensor_copy(bias[:], after[:, :1])
+            nc.gpsimd.memset(bias[:], 0.0)
+            for h in range(2):
+                s = hid.tile([P, 4, HALF], F32, name="silu")
+                nc.scalar.activation(s[:], banks.pop((e, 0, h))[:], SILU, bias=bias[:])
+                silus[e, h] = s
+
+        def gate_hidden(e):
+            hgs = []
+            for h in range(2):
+                hg = hid.tile([P, HALF * 4], BF16, name="hg", align_bytes=64)
+                nc.vector.tensor_tensor(
+                    hg[:].rearrange("p (c i t) -> p c t i", i=4, t=4),
+                    banks.pop((e, 1, h))[:].rearrange("p t (c i) -> p c t i", i=4),
+                    silus.pop((e, h))[:].rearrange("p t (c i) -> p c t i", i=4),
+                    MULT,
+                )
+                hgs.append(hg)
+            hc = keep.tile([P, C], U32, name="hc%d" % e, align_bytes=64)
+            hs = keep.tile([P, C], U8, name="hs%d" % e, align_bytes=64)
+            for h in range(2):
+                cols = slice(h * HALF, (h + 1) * HALF)
+                nc.vector.quantize_mx(out=hc[:, cols].bitcast(FP8X4), scales=hs[:, cols], in_=hgs[h][:])
+            hcodes[e] = (hc, hs)
+
+        def project(e):
+            hc, hs = hcodes.pop(e)
+            bank = py.tile([P, C], F32, name="ybank")
+            for h in range(2):
+                cols = slice(h * HALF, (h + 1) * HALF)
+                nc.tensor.matmul_mx(
+                    out=bank[:, cols],
+                    lhsT=w2codes[:, e * N : (e + 1) * N].bitcast(FP8X4),
+                    lhsT_scale=w2scale[:, e * N : (e + 1) * N],
+                    rhs=hc[:, cols].bitcast(FP8X4),
+                    rhs_scale=hs[:, cols],
+                    start=True,
+                    stop=True,
+                )
+            nc.scalar.copy(y_sb[:, e * C : (e + 1) * C], bank[:])
+
+        last = len(chunks) - 1
+        for i in range(len(chunks) + 6):
+            if i + loaded <= last:
+                load_w(i + loaded)
+                if i + loaded == 8 + PASSES:
+                    nc.sync.dma_start(pos1_sb[:], pos1)
+                    nc.sync.dma_start(pos2_sb[:], pos2)
+                    load_w2(0)
+                if i + loaded == last:
+                    load_w2(2)
+                    nc.sync.dma_start(gate_sb[:], gate.rearrange("r p t -> p r t"))
+            if i <= last:
+                regroup(i)
+            done = i - 1
+            if 0 <= done <= last:
+                quantise(done)
+                e, w, g = chunks[done]
+                if g == PASSES - 1:
+                    multiply(e, w)
+            if i <= last and chunks[i][1:] == (1, PASSES - 1):
+                activate(chunks[i][0], grouped[i])
+            ready = i - 3
+            if 0 <= ready <= last and chunks[ready][1:] == (1, PASSES - 1):
+                gate_hidden(chunks[ready][0])
+            ready = i - 4
+            if 0 <= ready <= last and chunks[ready][1:] == (1, PASSES - 1):
+                e = chunks[ready][0]
+                if e == 1:
+                    w2_prepare(0)
+                    project(0)
+                if e == 3:
+                    w2_prepare(2)
+                    project(2)
+                if e in (1, 3):
+                    project(e)
+
+        r1 = keep.tile([P, T], F32, name="r1")
+        r2 = keep.tile([P, T], F32, name="r2")
+        res = keep.tile([P, T], F32, name="res")
+        nc.vector.tensor_tensor(r1[:], y_sb[:].indirect(pos1_sb[:]), gate_sb[:, 0], MULT)
+        nc.vector.tensor_tensor(r2[:], y_sb[:].indirect(pos2_sb[:]), gate_sb[:, 1], MULT)
+        nc.vector.tensor_tensor(res[:], r1[:], r2[:], ADD)
+        nc.sync.dma_start(out, res[:])

@@ -19,8 +19,11 @@ PASSES = K // (P * J)
 HALF = 128
 PIECES = ((0, 384), (384, 704), (704, 1024))
 RAW_BUFS = 12
-SPLIT_M = 88
-VECTOR_CHUNKS = (6, 8, 10, 12, 14, 17, 19, 21)
+LAST_PARTS = 2
+VECTOR_CHUNKS = (0, 3, 4, 7, 10, 12, 15, 16)
+SPLIT = {18: 84, 19: 96, 21: 64, 22: 88, 23: 96}
+WARM = ((22, 3),)
+SILU_AFTER = (7, 13, 17, 22)
 
 
 def tile_routed_moe_kernel(tc, xT, w1, w3, w2, gate, offs, pos1, pos2, out):
@@ -72,15 +75,15 @@ def tile_routed_moe_kernel(tc, xT, w1, w3, w2, gate, offs, pos1, pos2, out):
             load_w(i)
         loaded = RAW_BUFS - PASSES
 
-        w2raw = []
+        w2raw = {}
 
         def load_w2(e0):
             raw = keep.tile([P, 2, J, N], F32, name="w2raw%d" % e0)
             nc.sync.dma_start(out=raw[:], in_=w2[e0 : e0 + 2].rearrange("e (p j) n -> p e j n", j=J))
-            w2raw.append(raw)
+            w2raw[e0] = raw
 
         def w2_prepare(e0):
-            raw = w2raw[e0 // 2]
+            raw = w2raw[e0]
             g4 = keep.tile([P, 2 * N * J], BF16, name="w2g%d" % e0, align_bytes=64)
             for k in range(2):
                 nc.scalar.copy(
@@ -111,9 +114,10 @@ def tile_routed_moe_kernel(tc, xT, w1, w3, w2, gate, offs, pos1, pos2, out):
             g4 = grp.tile([P, H * J], BF16, name="wg", tag="g4", align_bytes=64)
             dst = g4[:].rearrange("p (t m j) -> p m j t", t=4, j=J)
             src = raws.pop(i)[:].rearrange("p j (m t) -> p m j t", t=4)
-            if i == len(chunks) - 1:
-                nc.vector.tensor_copy(dst[:, :SPLIT_M], src[:, :SPLIT_M])
-                nc.scalar.copy(dst[:, SPLIT_M:], src[:, SPLIT_M:])
+            if i in SPLIT:
+                m = SPLIT[i]
+                nc.vector.tensor_copy(dst[:, :m], src[:, :m])
+                nc.scalar.copy(dst[:, m:], src[:, m:])
             elif i in VECTOR_CHUNKS:
                 nc.vector.tensor_copy(dst, src)
             else:
@@ -127,7 +131,14 @@ def tile_routed_moe_kernel(tc, xT, w1, w3, w2, gate, offs, pos1, pos2, out):
                 ws = codes.tile([P, PASSES, H], U8, name="ws", align_bytes=64)
                 wq[e, w] = (wc, ws)
             wc, ws = wq[e, w]
-            nc.vector.quantize_mx(out=wc[:, g].bitcast(FP8X4), scales=ws[:, g], in_=grouped.pop(i)[:])
+            g4 = grouped.pop(i)
+            parts = LAST_PARTS if i == len(chunks) - 1 else 1
+            width = H // parts
+            for k in range(parts):
+                cols = slice(k * width, (k + 1) * width)
+                nc.vector.quantize_mx(
+                    out=wc[:, g, cols].bitcast(FP8X4), scales=ws[:, g, cols], in_=g4[:, k * width * J : (k + 1) * width * J]
+                )
 
         banks = {}
 
@@ -180,57 +191,63 @@ def tile_routed_moe_kernel(tc, xT, w1, w3, w2, gate, offs, pos1, pos2, out):
                 nc.vector.quantize_mx(out=hc[:, cols].bitcast(FP8X4), scales=hs[:, cols], in_=hgs[h][:])
             hcodes[e] = (hc, hs)
 
-        def project(e):
-            hc, hs = hcodes.pop(e)
-            bank = py.tile([P, C], F32, name="ybank")
-            for h in range(2):
-                cols = slice(h * HALF, (h + 1) * HALF)
-                nc.tensor.matmul_mx(
-                    out=bank[:, cols],
-                    lhsT=w2codes[:, e * N : (e + 1) * N].bitcast(FP8X4),
-                    lhsT_scale=w2scale[:, e * N : (e + 1) * N],
-                    rhs=hc[:, cols].bitcast(FP8X4),
-                    rhs_scale=hs[:, cols],
-                    start=True,
-                    stop=True,
-                )
-            nc.scalar.copy(y_sb[:, e * C : (e + 1) * C], bank[:])
+        def project(bank, experts):
+            for k, e in enumerate(experts):
+                hc, hs = hcodes.pop(e)
+                for h in range(2):
+                    cols = slice(h * HALF, (h + 1) * HALF)
+                    nc.tensor.matmul_mx(
+                        out=bank[:, 2 * k + h],
+                        lhsT=w2codes[:, e * N : (e + 1) * N].bitcast(FP8X4),
+                        lhsT_scale=w2scale[:, e * N : (e + 1) * N],
+                        rhs=hc[:, cols].bitcast(FP8X4),
+                        rhs_scale=hs[:, cols],
+                        start=True,
+                        stop=True,
+                    )
+            n = 2 * len(experts)
+            nc.scalar.copy(
+                y_sb[:, experts[0] * C : experts[0] * C + n * HALF].rearrange("p (h c) -> p h c", c=HALF), bank[:, :n]
+            )
 
         last = len(chunks) - 1
         for i in range(len(chunks) + 6):
             if i + loaded <= last:
                 load_w(i + loaded)
-                if i + loaded == 8 + PASSES:
-                    nc.sync.dma_start(pos1_sb[:], pos1)
-                    nc.sync.dma_start(pos2_sb[:], pos2)
-                    load_w2(0)
                 if i + loaded == last:
                     load_w2(2)
+                    load_w2(0)
+                    nc.sync.dma_start(pos1_sb[:], pos1)
+                    nc.sync.dma_start(pos2_sb[:], pos2)
                     nc.sync.dma_start(gate_sb[:], gate.rearrange("r p t -> p r t"))
             if i <= last:
                 regroup(i)
+                for at, count in WARM:
+                    if at == i:
+                        idle = py.tile([P, 512], F32, name="ybank")
+                        for r in range(count):
+                            nc.tensor.matmul(idle[:], grouped[i][:, :P], grouped[i][:, 512:1024], start=True, stop=True)
             done = i - 1
             if 0 <= done <= last:
                 quantise(done)
                 e, w, g = chunks[done]
                 if g == PASSES - 1:
                     multiply(e, w)
-            if i <= last and chunks[i][1:] == (1, PASSES - 1):
-                activate(chunks[i][0], grouped[i])
-            ready = i - 3
-            if 0 <= ready <= last and chunks[ready][1:] == (1, PASSES - 1):
-                gate_hidden(chunks[ready][0])
+            for e, at in enumerate(SILU_AFTER):
+                if at == i:
+                    activate(e, grouped[i])
             ready = i - 4
             if 0 <= ready <= last and chunks[ready][1:] == (1, PASSES - 1):
-                e = chunks[ready][0]
-                if e == 1:
-                    w2_prepare(0)
-                    project(0)
-                if e == 3:
-                    w2_prepare(2)
-                    project(2)
-                if e in (1, 3):
-                    project(e)
+                gate_hidden(chunks[ready][0])
+            if i == last + 1:
+                w2_prepare(2)
+                w2_prepare(0)
+        ybank = py.tile([P, 4, HALF], F32, name="ybank")
+        project(ybank, (0, 1))
+        ybank = py.tile([P, 4, HALF], F32, name="ybank")
+        project(ybank, (2,))
+        bank0 = pa.tile([P, 4, HALF], F32, name="bank0")
+        project(bank0, (3,))
 
         r1 = keep.tile([P, T], F32, name="r1")
         r2 = keep.tile([P, T], F32, name="r2")

@@ -17,13 +17,18 @@ P = 128
 J = 4
 PASSES = K // (P * J)
 HALF = 128
+CHUNKS = 2 * PASSES
+LAST = E * CHUNKS - 1
 PIECES = ((0, 384), (384, 704), (704, 1024))
-RAW_BUFS = 12
-LAST_PARTS = 2
-VECTOR_CHUNKS = (0, 3, 4, 7, 10, 12, 15, 16)
-SPLIT = {18: 84, 19: 96, 21: 64, 22: 88, 23: 96}
-WARM = ((22, 3),)
-SILU_AFTER = (7, 13, 17, 22)
+RAW_BUFS = 10
+VECTOR_X = (80, 0, 0)
+VECTOR_M = (64, 32, 64, 0, 32, 0, 0, 64, 64, 48, 32, 128, 48, 0, 48, 128, 48, 48, 128, 64, 0, 48, 64, 128)
+PAIRS = (0, 2, 4, 6, 8, 14, 16)
+SILU_AFTER = (8, 13, 17, 22)
+WARM = ()
+GATHER_AT = {2: 1, 8: 2}
+LAST_PARTS = 4
+HIDDEN_LAG = 3
 
 
 def tile_routed_moe_kernel(tc, xT, w1, w3, w2, gate, offs, pos1, pos2, out):
@@ -31,8 +36,8 @@ def tile_routed_moe_kernel(tc, xT, w1, w3, w2, gate, offs, pos1, pos2, out):
     with (
         tc.tile_pool(name="keep", bufs=1) as keep,
         tc.tile_pool(name="raw", bufs=RAW_BUFS) as rawp,
-        tc.tile_pool(name="grouped", bufs=8) as grp,
-        tc.tile_pool(name="codes", bufs=4) as codes,
+        tc.tile_pool(name="grouped", bufs=5) as grp,
+        tc.tile_pool(name="codes", bufs=3) as codes,
         tc.tile_pool(name="hid", bufs=4) as hid,
         tc.psum_pool(name="pa", bufs=3) as pa,
         tc.psum_pool(name="pb", bufs=3) as pb,
@@ -55,14 +60,13 @@ def tile_routed_moe_kernel(tc, xT, w1, w3, w2, gate, offs, pos1, pos2, out):
         nc.scalar.activation(warm[:], warm[:], SILU)
         nc.gpsimd.memset(xscale[:], 0)
 
-        chunks = [(e, w, g) for e in range(E) for w in range(2) for g in range(PASSES)]
         raws = {}
 
         def load_w(i):
-            e, w, g = chunks[i]
+            e, c = divmod(i, CHUNKS)
+            w, g = divmod(c, PASSES)
             raw = rawp.tile([P, J, H], F32, name="raw")
-            src = (w1, w3)[w][e].rearrange("(g p j) c -> g p j c", p=P, j=J)[g]
-            nc.sync.dma_start(out=raw[:], in_=src)
+            nc.sync.dma_start(out=raw[:], in_=(w1, w3)[w][e].rearrange("(g p j) c -> g p j c", p=P, j=J)[g])
             raws[i] = raw
 
         nc.sync.dma_start(offs_sb[:], offs)
@@ -71,14 +75,14 @@ def tile_routed_moe_kernel(tc, xT, w1, w3, w2, gate, offs, pos1, pos2, out):
             raw = rawp.tile([P, J, T], F32, name="raw")
             nc.sync.dma_start(out=raw[:], in_=xT.rearrange("(g p j) n -> g p j n", p=P, j=J)[g])
             xraw.append(raw)
-        for i in range(RAW_BUFS - PASSES):
+        ahead = RAW_BUFS - PASSES
+        for i in range(ahead):
             load_w(i)
-        loaded = RAW_BUFS - PASSES
 
         w2raw = {}
 
         def load_w2(e0):
-            raw = keep.tile([P, 2, J, N], F32, name="w2raw%d" % e0)
+            raw = rawp.tile([P, 2, J, N], F32, name="w2raw", tag="raw")
             nc.sync.dma_start(out=raw[:], in_=w2[e0 : e0 + 2].rearrange("e (p j) n -> p e j n", j=J))
             w2raw[e0] = raw
 
@@ -93,67 +97,86 @@ def tile_routed_moe_kernel(tc, xT, w1, w3, w2, gate, offs, pos1, pos2, out):
             cols = slice(e0 * N, (e0 + 2) * N)
             nc.vector.quantize_mx(out=w2codes[:, cols].bitcast(FP8X4), scales=w2scale[:, cols], in_=g4[:])
 
+        def share(dst, src, n):
+            if n > 0:
+                nc.vector.tensor_copy(dst[:, :n], src[:, :n])
+            if n < dst.shape[1]:
+                nc.scalar.copy(dst[:, n:], src[:, n:])
+
+        def gather_codes(g, n):
+            a, b = PIECES[n]
+            nc.vector.tensor_copy(scodes[g][:, a:b], xcodes[g][:].indirect(offs_sb[:, a // 16 : b // 16]))
+
+        def gather_scales(n):
+            a, b = PIECES[n]
+            nc.vector.tensor_copy(sscale[:, a:b], xscale[:].indirect(offs_sb[:, a // 16 : b // 16]))
+
         for g in range(PASSES):
             g4 = grp.tile([P, T * J], BF16, name="xg", tag="g4", align_bytes=64)
-            dst = g4[:].rearrange("p (c i j) -> p c j i", i=4, j=J)
-            src = xraw[g][:].rearrange("p j (c i) -> p c j i", i=4)
-            if g == 0:
-                nc.vector.tensor_copy(dst, src)
-            else:
-                nc.scalar.copy(dst, src)
+            share(
+                g4[:].rearrange("p (c i j) -> p c j i", i=4, j=J),
+                xraw[g][:].rearrange("p j (c i) -> p c j i", i=4),
+                VECTOR_X[g],
+            )
             nc.vector.quantize_mx(out=xcodes[g][:].bitcast(FP8X4), scales=xscale[4 * g : P, :], in_=g4[:])
-            for a, b in PIECES:
-                nc.vector.tensor_copy(scodes[g][:, a:b], xcodes[g][:].indirect(offs_sb[:, a // 16 : b // 16]))
-        for a, b in PIECES:
-            nc.vector.tensor_copy(sscale[:, a:b], xscale[:].indirect(offs_sb[:, a // 16 : b // 16]))
+            for n in range(len(PIECES)):
+                if n not in GATHER_AT.values():
+                    gather_codes(g, n)
+        for n in range(len(PIECES)):
+            if n not in GATHER_AT.values():
+                gather_scales(n)
 
         grouped = {}
         wq = {}
 
         def regroup(i):
-            g4 = grp.tile([P, H * J], BF16, name="wg", tag="g4", align_bytes=64)
-            dst = g4[:].rearrange("p (t m j) -> p m j t", t=4, j=J)
-            src = raws.pop(i)[:].rearrange("p j (m t) -> p m j t", t=4)
-            if i in SPLIT:
-                m = SPLIT[i]
-                nc.vector.tensor_copy(dst[:, :m], src[:, :m])
-                nc.scalar.copy(dst[:, m:], src[:, m:])
-            elif i in VECTOR_CHUNKS:
-                nc.vector.tensor_copy(dst, src)
+            if i % 2 and i - 1 in PAIRS:
+                g4 = grouped[i - 1][0][:, H * J :]
             else:
-                nc.scalar.copy(dst, src)
-            grouped[i] = g4
+                tile = grp.tile([P, (1 + (i in PAIRS)) * H * J], BF16, name="wg", tag="g4", align_bytes=64)
+                g4 = tile[:]
+            mine = g4[:, : H * J]
+            n = VECTOR_M[i]
+            dst = mine.rearrange("p (a b m j) -> p a m j b", a=2, b=2, j=J)
+            src = raws.pop(i)[:].rearrange("p j (m a b) -> p a m j b", a=2, b=2)
+            if n > 0:
+                nc.vector.tensor_copy(dst[:, :, :n], src[:, :, :n])
+            if n < 128:
+                nc.scalar.copy(dst[:, :, n:], src[:, :, n:])
+            grouped[i] = (g4, mine)
 
         def quantise(i):
-            e, w, g = chunks[i]
-            if g == 0:
-                wc = codes.tile([P, PASSES, H], U32, name="wc", align_bytes=64)
-                ws = codes.tile([P, PASSES, H], U8, name="ws", align_bytes=64)
-                wq[e, w] = (wc, ws)
-            wc, ws = wq[e, w]
-            g4 = grouped.pop(i)
-            parts = LAST_PARTS if i == len(chunks) - 1 else 1
-            width = H // parts
+            e, c = divmod(i, CHUNKS)
+            if c == 0:
+                wc = codes.tile([P, CHUNKS * H], U32, name="wc", align_bytes=64)
+                ws = codes.tile([P, CHUNKS * H], U8, name="ws", align_bytes=64)
+                wq[e] = (wc, ws)
+            wc, ws = wq[e]
+            width = (1 + (i in PAIRS)) * H
+            parts = LAST_PARTS if i == LAST else 1
+            step = width // parts
             for k in range(parts):
-                cols = slice(k * width, (k + 1) * width)
+                cols = slice(c * H + k * step, c * H + (k + 1) * step)
                 nc.vector.quantize_mx(
-                    out=wc[:, g, cols].bitcast(FP8X4), scales=ws[:, g, cols], in_=g4[:, k * width * J : (k + 1) * width * J]
+                    out=wc[:, cols].bitcast(FP8X4),
+                    scales=ws[:, cols],
+                    in_=grouped[i][0][:, k * step * J : (k + 1) * step * J],
                 )
 
         banks = {}
 
         def multiply(e, w):
-            wc, ws = wq.pop((e, w))
+            wc, ws = wq[e]
             for h in range(2):
                 bank = (pa, pb)[w].tile([P, 4, HALF], F32, name="bank%d" % w)
                 cols = slice(e * C + h * HALF, e * C + (h + 1) * HALF)
                 for t in range(4):
-                    rows = slice(t * P, (t + 1) * P)
                     for g in range(PASSES):
+                        first = (w * PASSES + g) * H + t * P
                         nc.tensor.matmul_mx(
                             out=bank[:, t],
-                            lhsT=wc[:, g, rows].bitcast(FP8X4),
-                            lhsT_scale=ws[:, g, rows],
+                            lhsT=wc[:, first : first + P].bitcast(FP8X4),
+                            lhsT_scale=ws[:, first : first + P],
                             rhs=scodes[g][:, cols].bitcast(FP8X4),
                             rhs_scale=sscale[4 * g : P, cols],
                             start=(g == 0),
@@ -165,30 +188,32 @@ def tile_routed_moe_kernel(tc, xT, w1, w3, w2, gate, offs, pos1, pos2, out):
         hcodes = {}
 
         def activate(e, after):
-            bias = hid.tile([P, 1], F32, name="bias")
-            nc.gpsimd.tensor_copy(bias[:], after[:, :1])
+            bias = hid.tile([P, 2], F32, name="bias")
+            nc.gpsimd.tensor_copy(bias[:], after[:, 0:512:511])
             nc.gpsimd.memset(bias[:], 0.0)
             for h in range(2):
                 s = hid.tile([P, 4, HALF], F32, name="silu")
-                nc.scalar.activation(s[:], banks.pop((e, 0, h))[:], SILU, bias=bias[:])
+                nc.scalar.activation(s[:], banks.pop((e, 0, h))[:], SILU, bias=bias[:, :1])
                 silus[e, h] = s
 
         def gate_hidden(e):
-            hgs = []
+            hc = keep.tile([P, C], U32, name="hc%d" % e, align_bytes=64)
+            hs = keep.tile([P, C], U8, name="hs%d" % e, align_bytes=64)
+            hg = hid.tile([P, C * 4], BF16, name="hg", align_bytes=64)
             for h in range(2):
-                hg = hid.tile([P, HALF * 4], BF16, name="hg", align_bytes=64)
                 nc.vector.tensor_tensor(
-                    hg[:].rearrange("p (c i t) -> p c t i", i=4, t=4),
+                    hg[:, h * HALF * 4 : (h + 1) * HALF * 4].rearrange("p (c i t) -> p c t i", i=4, t=4),
                     banks.pop((e, 1, h))[:].rearrange("p t (c i) -> p c t i", i=4),
                     silus.pop((e, h))[:].rearrange("p t (c i) -> p c t i", i=4),
                     MULT,
                 )
-                hgs.append(hg)
-            hc = keep.tile([P, C], U32, name="hc%d" % e, align_bytes=64)
-            hs = keep.tile([P, C], U8, name="hs%d" % e, align_bytes=64)
-            for h in range(2):
-                cols = slice(h * HALF, (h + 1) * HALF)
-                nc.vector.quantize_mx(out=hc[:, cols].bitcast(FP8X4), scales=hs[:, cols], in_=hgs[h][:])
+            parts = 2 if e == E - 1 else 1
+            step = C // parts
+            for k in range(parts):
+                cols = slice(k * step, (k + 1) * step)
+                nc.vector.quantize_mx(
+                    out=hc[:, cols].bitcast(FP8X4), scales=hs[:, cols], in_=hg[:, k * step * 4 : (k + 1) * step * 4]
+                )
             hcodes[e] = (hc, hs)
 
         def project(bank, experts):
@@ -210,36 +235,45 @@ def tile_routed_moe_kernel(tc, xT, w1, w3, w2, gate, offs, pos1, pos2, out):
                 y_sb[:, experts[0] * C : experts[0] * C + n * HALF].rearrange("p (h c) -> p h c", c=HALF), bank[:, :n]
             )
 
-        last = len(chunks) - 1
-        for i in range(len(chunks) + 6):
-            if i + loaded <= last:
-                load_w(i + loaded)
-                if i + loaded == last:
+        for i in range(LAST + 1 + HIDDEN_LAG):
+            if i + ahead <= LAST:
+                load_w(i + ahead)
+                if i + ahead == LAST:
                     load_w2(2)
                     load_w2(0)
                     nc.sync.dma_start(pos1_sb[:], pos1)
                     nc.sync.dma_start(pos2_sb[:], pos2)
                     nc.sync.dma_start(gate_sb[:], gate.rearrange("r p t -> p r t"))
-            if i <= last:
+            if i in GATHER_AT:
+                for g in range(PASSES):
+                    gather_codes(g, GATHER_AT[i])
+                gather_scales(GATHER_AT[i])
+            if i <= LAST:
                 regroup(i)
                 for at, count in WARM:
                     if at == i:
-                        idle = py.tile([P, 512], F32, name="ybank")
+                        idle = py.tile([P, 4, HALF], F32, name="ybank")
                         for r in range(count):
-                            nc.tensor.matmul(idle[:], grouped[i][:, :P], grouped[i][:, 512:1024], start=True, stop=True)
+                            nc.tensor.matmul(
+                                idle[:].rearrange("p t c -> p (t c)"),
+                                grouped[i][1][:, :P],
+                                grouped[i][1][:, 512:1024],
+                                start=True,
+                                stop=True,
+                            )
             done = i - 1
-            if 0 <= done <= last:
-                quantise(done)
-                e, w, g = chunks[done]
-                if g == PASSES - 1:
-                    multiply(e, w)
+            if 0 <= done <= LAST and done not in PAIRS:
+                quantise(done - 1 if done - 1 in PAIRS else done)
+                for c in ((done - 1, done) if done - 1 in PAIRS else (done,)):
+                    if c % PASSES == PASSES - 1:
+                        multiply(c // CHUNKS, c % CHUNKS // PASSES)
             for e, at in enumerate(SILU_AFTER):
                 if at == i:
-                    activate(e, grouped[i])
-            ready = i - 4
-            if 0 <= ready <= last and chunks[ready][1:] == (1, PASSES - 1):
-                gate_hidden(chunks[ready][0])
-            if i == last + 1:
+                    activate(e, grouped[i][1])
+            ready = i - HIDDEN_LAG
+            if 0 <= ready <= LAST and ready % CHUNKS == CHUNKS - 1:
+                gate_hidden(ready // CHUNKS)
+            if i == LAST + 1:
                 w2_prepare(2)
                 w2_prepare(0)
         ybank = py.tile([P, 4, HALF], F32, name="ybank")

import concourse.mybir as mybir

K, T, E, C, H, N = 1536, 512, 4, 256, 512, 128
FLOPS = 2 * E * C * H * (2 * K + N)

F32 = mybir.dt.float32
BF16 = mybir.dt.bfloat16
U32 = mybir.dt.uint32
U16 = mybir.dt.uint16
U8 = mybir.dt.uint8
FP8X4 = mybir.dt.float8_e4m3fn_x4
SILU = mybir.ActivationFunctionType.Silu
MULT = mybir.AluOpType.mult
ADD = mybir.AluOpType.add

P = 128
J = 4
PASSES = K // (P * J)
HALF = 128
CHUNKS = 2 * PASSES
LAST = E * CHUNKS - 1
PIECES = ((0, 384), (384, 704), (704, 1024))
RAW_BUFS = 10
VECTOR_X = (80, 0, 0)
VECTOR_M = (64, 32, 64, 0, 32, 0, 0, 64, 64, 48, 32, 128, 48, 0, 48, 128, 48, 48, 128, 64, 0, 48, 64, 128)
PAIRS = (0, 2, 4, 6, 8, 14, 16)
SILU_AFTER = (8, 13, 17, 22)
WARM = ()
GATHER_AT = {2: 1, 8: 2}
LAST_PARTS = 4
HIDDEN_LAG = 3


def tile_routed_moe_kernel(tc, xT, w1, w3, w2, gate, offs, pos1, pos2, out):
    nc = tc.nc
    with (
        tc.tile_pool(name="keep", bufs=1) as keep,
        tc.tile_pool(name="raw", bufs=RAW_BUFS) as rawp,
        tc.tile_pool(name="grouped", bufs=5) as grp,
        tc.tile_pool(name="codes", bufs=3) as codes,
        tc.tile_pool(name="hid", bufs=4) as hid,
        tc.psum_pool(name="pa", bufs=3) as pa,
        tc.psum_pool(name="pb", bufs=3) as pb,
        tc.psum_pool(name="py", bufs=2) as py,
    ):
        offs_sb = keep.tile([P, E * C // 16], U16, name="offs_sb")
        pos1_sb = keep.tile([P, T // 16], U16, name="pos1_sb")
        pos2_sb = keep.tile([P, T // 16], U16, name="pos2_sb")
        gate_sb = keep.tile([P, 2, T], F32, name="gate_sb")
        y_sb = keep.tile([P, E * C], F32, name="y_sb")
        xcodes = [keep.tile([P, T], U32, name="xc%d" % g, align_bytes=64) for g in range(PASSES)]
        xscale = keep.tile([P, T], U8, name="xscale", align_bytes=64)
        scodes = [keep.tile([P, E * C], U32, name="sc%d" % g, align_bytes=64) for g in range(PASSES)]
        sscale = keep.tile([P, E * C], U8, name="sscale", align_bytes=64)
        w2codes = keep.tile([P, E * N], U32, name="w2codes", align_bytes=64)
        w2scale = keep.tile([P, E * N], U8, name="w2scale", align_bytes=64)
        warm = keep.tile([P, 8], F32, name="warm")

        nc.gpsimd.memset(warm[:], 0.0)
        nc.scalar.activation(warm[:], warm[:], SILU)
        nc.gpsimd.memset(xscale[:], 0)

        raws = {}

        def load_w(i):
            e, c = divmod(i, CHUNKS)
            w, g = divmod(c, PASSES)
            raw = rawp.tile([P, J, H], F32, name="raw")
            nc.sync.dma_start(out=raw[:], in_=(w1, w3)[w][e].rearrange("(g p j) c -> g p j c", p=P, j=J)[g])
            raws[i] = raw

        nc.sync.dma_start(offs_sb[:], offs)
        xraw = []
        for g in range(PASSES):
            raw = rawp.tile([P, J, T], F32, name="raw")
            nc.sync.dma_start(out=raw[:], in_=xT.rearrange("(g p j) n -> g p j n", p=P, j=J)[g])
            xraw.append(raw)
        ahead = RAW_BUFS - PASSES
        for i in range(ahead):
            load_w(i)

        w2raw = {}

        def load_w2(e0):
            raw = rawp.tile([P, 2, J, N], F32, name="w2raw", tag="raw")
            nc.sync.dma_start(out=raw[:], in_=w2[e0 : e0 + 2].rearrange("e (p j) n -> p e j n", j=J))
            w2raw[e0] = raw

        def w2_prepare(e0):
            raw = w2raw[e0]
            g4 = keep.tile([P, 2 * N * J], BF16, name="w2g%d" % e0, align_bytes=64)
            for k in range(2):
                nc.scalar.copy(
                    g4[:, k * N * J : (k + 1) * N * J].rearrange("p (c i j) -> p c j i", i=4, j=J),
                    raw[:, k].rearrange("p j (c i) -> p c j i", i=4),
                )
            cols = slice(e0 * N, (e0 + 2) * N)
            nc.vector.quantize_mx(out=w2codes[:, cols].bitcast(FP8X4), scales=w2scale[:, cols], in_=g4[:])

        def share(dst, src, n):
            if n > 0:
                nc.vector.tensor_copy(dst[:, :n], src[:, :n])
            if n < dst.shape[1]:
                nc.scalar.copy(dst[:, n:], src[:, n:])

        def gather_codes(g, n):
            a, b = PIECES[n]
            nc.vector.tensor_copy(scodes[g][:, a:b], xcodes[g][:].indirect(offs_sb[:, a // 16 : b // 16]))

        def gather_scales(n):
            a, b = PIECES[n]
            nc.vector.tensor_copy(sscale[:, a:b], xscale[:].indirect(offs_sb[:, a // 16 : b // 16]))

        for g in range(PASSES):
            g4 = grp.tile([P, T * J], BF16, name="xg", tag="g4", align_bytes=64)
            share(
                g4[:].rearrange("p (c i j) -> p c j i", i=4, j=J),
                xraw[g][:].rearrange("p j (c i) -> p c j i", i=4),
                VECTOR_X[g],
            )
            nc.vector.quantize_mx(out=xcodes[g][:].bitcast(FP8X4), scales=xscale[4 * g : P, :], in_=g4[:])
            for n in range(len(PIECES)):
                if n not in GATHER_AT.values():
                    gather_codes(g, n)
        for n in range(len(PIECES)):
            if n not in GATHER_AT.values():
                gather_scales(n)

        grouped = {}
        wq = {}

        def regroup(i):
            if i % 2 and i - 1 in PAIRS:
                g4 = grouped[i - 1][0][:, H * J :]
            else:
                tile = grp.tile([P, (1 + (i in PAIRS)) * H * J], BF16, name="wg", tag="g4", align_bytes=64)
                g4 = tile[:]
            mine = g4[:, : H * J]
            n = VECTOR_M[i]
            dst = mine.rearrange("p (a b m j) -> p a m j b", a=2, b=2, j=J)
            src = raws.pop(i)[:].rearrange("p j (m a b) -> p a m j b", a=2, b=2)
            if n > 0:
                nc.vector.tensor_copy(dst[:, :, :n], src[:, :, :n])
            if n < 128:
                nc.scalar.copy(dst[:, :, n:], src[:, :, n:])
            grouped[i] = (g4, mine)

        def quantise(i):
            e, c = divmod(i, CHUNKS)
            if c == 0:
                wc = codes.tile([P, CHUNKS * H], U32, name="wc", align_bytes=64)
                ws = codes.tile([P, CHUNKS * H], U8, name="ws", align_bytes=64)
                wq[e] = (wc, ws)
            wc, ws = wq[e]
            width = (1 + (i in PAIRS)) * H
            parts = LAST_PARTS if i == LAST else 1
            step = width // parts
            for k in range(parts):
                cols = slice(c * H + k * step, c * H + (k + 1) * step)
                nc.vector.quantize_mx(
                    out=wc[:, cols].bitcast(FP8X4),
                    scales=ws[:, cols],
                    in_=grouped[i][0][:, k * step * J : (k + 1) * step * J],
                )

        banks = {}

        def multiply(e, w):
            wc, ws = wq[e]
            for h in range(2):
                bank = (pa, pb)[w].tile([P, 4, HALF], F32, name="bank%d" % w)
                cols = slice(e * C + h * HALF, e * C + (h + 1) * HALF)
                for t in range(4):
                    for g in range(PASSES):
                        first = (w * PASSES + g) * H + t * P
                        nc.tensor.matmul_mx(
                            out=bank[:, t],
                            lhsT=wc[:, first : first + P].bitcast(FP8X4),
                            lhsT_scale=ws[:, first : first + P],
                            rhs=scodes[g][:, cols].bitcast(FP8X4),
                            rhs_scale=sscale[4 * g : P, cols],
                            start=(g == 0),
                            stop=(g == PASSES - 1),
                        )
                banks[e, w, h] = bank

        silus = {}
        hcodes = {}

        def activate(e, after):
            bias = hid.tile([P, 2], F32, name="bias")
            nc.gpsimd.tensor_copy(bias[:], after[:, 0:512:511])
            nc.gpsimd.memset(bias[:], 0.0)
            for h in range(2):
                s = hid.tile([P, 4, HALF], F32, name="silu")
                nc.scalar.activation(s[:], banks.pop((e, 0, h))[:], SILU, bias=bias[:, :1])
                silus[e, h] = s

        def gate_hidden(e):
            hc = keep.tile([P, C], U32, name="hc%d" % e, align_bytes=64)
            hs = keep.tile([P, C], U8, name="hs%d" % e, align_bytes=64)
            hg = hid.tile([P, C * 4], BF16, name="hg", align_bytes=64)
            for h in range(2):
                nc.vector.tensor_tensor(
                    hg[:, h * HALF * 4 : (h + 1) * HALF * 4].rearrange("p (c i t) -> p c t i", i=4, t=4),
                    banks.pop((e, 1, h))[:].rearrange("p t (c i) -> p c t i", i=4),
                    silus.pop((e, h))[:].rearrange("p t (c i) -> p c t i", i=4),
                    MULT,
                )
            parts = 2 if e == E - 1 else 1
            step = C // parts
            for k in range(parts):
                cols = slice(k * step, (k + 1) * step)
                nc.vector.quantize_mx(
                    out=hc[:, cols].bitcast(FP8X4), scales=hs[:, cols], in_=hg[:, k * step * 4 : (k + 1) * step * 4]
                )
            hcodes[e] = (hc, hs)

        def project(bank, experts):
            for k, e in enumerate(experts):
                hc, hs = hcodes.pop(e)
                for h in range(2):
                    cols = slice(h * HALF, (h + 1) * HALF)
                    nc.tensor.matmul_mx(
                        out=bank[:, 2 * k + h],
                        lhsT=w2codes[:, e * N : (e + 1) * N].bitcast(FP8X4),
                        lhsT_scale=w2scale[:, e * N : (e + 1) * N],
                        rhs=hc[:, cols].bitcast(FP8X4),
                        rhs_scale=hs[:, cols],
                        start=True,
                        stop=True,
                    )
            n = 2 * len(experts)
            nc.scalar.copy(
                y_sb[:, experts[0] * C : experts[0] * C + n * HALF].rearrange("p (h c) -> p h c", c=HALF), bank[:, :n]
            )

        for i in range(LAST + 1 + HIDDEN_LAG):
            if i + ahead <= LAST:
                load_w(i + ahead)
                if i + ahead == LAST:
                    load_w2(2)
                    load_w2(0)
                    nc.sync.dma_start(pos1_sb[:], pos1)
                    nc.sync.dma_start(pos2_sb[:], pos2)
                    nc.sync.dma_start(gate_sb[:], gate.rearrange("r p t -> p r t"))
            if i in GATHER_AT:
                for g in range(PASSES):
                    gather_codes(g, GATHER_AT[i])
                gather_scales(GATHER_AT[i])
            if i <= LAST:
                regroup(i)
                for at, count in WARM:
                    if at == i:
                        idle = py.tile([P, 4, HALF], F32, name="ybank")
                        for r in range(count):
                            nc.tensor.matmul(
                                idle[:].rearrange("p t c -> p (t c)"),
                                grouped[i][1][:, :P],
                                grouped[i][1][:, 512:1024],
                                start=True,
                                stop=True,
                            )
            done = i - 1
            if 0 <= done <= LAST and done not in PAIRS:
                quantise(done - 1 if done - 1 in PAIRS else done)
                for c in ((done - 1, done) if done - 1 in PAIRS else (done,)):
                    if c % PASSES == PASSES - 1:
                        multiply(c // CHUNKS, c % CHUNKS // PASSES)
            for e, at in enumerate(SILU_AFTER):
                if at == i:
                    activate(e, grouped[i][1])
            ready = i - HIDDEN_LAG
            if 0 <= ready <= LAST and ready % CHUNKS == CHUNKS - 1:
                gate_hidden(ready // CHUNKS)
            if i == LAST + 1:
                w2_prepare(2)
                w2_prepare(0)
        ybank = py.tile([P, 4, HALF], F32, name="ybank")
        project(ybank, (0, 1))
        ybank = py.tile([P, 4, HALF], F32, name="ybank")
        project(ybank, (2,))
        bank0 = pa.tile([P, 4, HALF], F32, name="bank0")
        project(bank0, (3,))

        r1 = keep.tile([P, T], F32, name="r1")
        r2 = keep.tile([P, T], F32, name="r2")
        res = keep.tile([P, T], F32, name="res")
        nc.vector.tensor_tensor(r1[:], y_sb[:].indirect(pos1_sb[:]), gate_sb[:, 0], MULT)
        nc.vector.tensor_tensor(r2[:], y_sb[:].indirect(pos2_sb[:]), gate_sb[:, 1], MULT)
        nc.vector.tensor_tensor(res[:], r1[:], r2[:], ADD)
        nc.sync.dma_start(out, res[:])
